import numpy as np, ml_dtypes
CORES = [3,11,19,27,35,43,51,59]
N = 8
import mx_ref
BF = ml_dtypes.bfloat16
def gentries(a):
    return np.ascontiguousarray(a.reshape(8, 16, -1).transpose(0, 2, 1)).reshape(8, -1)
def gtable(e):
    e = np.asarray(e); return np.ascontiguousarray(e.reshape(8, -1, 16).transpose(0, 2, 1)).reshape(128, -1).astype(np.int32)
def gcols(t, e):
    v = np.concatenate([t.reshape(8, 16, -1, 4), np.zeros((8, 16, 1, 4), BF)], axis=2)
    return np.ascontiguousarray(np.stack([v[g][:, e[g]] for g in range(8)])).reshape(128, -1)
def tile(rs):
    return np.stack(rs, axis=2).reshape(128, -1).astype(BF)
def pick(q, e):
    c = np.concatenate([q[0].reshape(128, -1, 4), np.zeros((128, 1, 4), np.uint8)], axis=1); s = np.concatenate([q[1], np.ones((16, 1), np.uint8)], axis=1)
    return (np.ascontiguousarray(c[:, e].reshape(128, -1)), np.ascontiguousarray(s[:, e]))
def join(*qs):
    return (np.concatenate([q[0] for q in qs], axis=1), np.concatenate([q[1] for q in qs], axis=1))
def put(q, e, v):
    c, s = q[0].reshape(128, -1, 4).copy(), q[1].copy(); c[:, e] = v[0].reshape(128, -1, 4); s[:, e] = v[1]
    return (c.reshape(128, -1), s)
def pk(c, s):
    return (np.ascontiguousarray(c), mx_ref.live(s))
def emit(q):
    return q[0], q[1]
def packed(v, rng):
    q = [mx_ref.quantize(np.ascontiguousarray(v[r])) for r in range(N)]
    return np.stack([a for a, b in q]), np.stack([mx_ref.plane(b, rng) for a, b in q])
def values_of_codes():
    e, c = np.zeros((128, 128, 4), np.float32), np.zeros((128, 2, 4), np.uint8)
    e[np.arange(128), np.arange(128), 0] = 1
    c[:127, :, 0] = np.arange(256).reshape(2, 128).T[:127]
    return mx_ref.matmul(mx_ref.quantize(e.reshape(128, 512).astype(BF)), (c.reshape(128, 8), np.full((16, 2), 127, np.uint8))).T.reshape(-1).astype(np.float64)
CODE_VALUE, SCALE_VALUE = values_of_codes(), 2.0 ** (np.arange(256) - 127.0)
def decode(q):
    return (CODE_VALUE[q[0]].reshape(16, 8, -1, 4) * SCALE_VALUE[q[1]][:, None, :, None] + 0.0).reshape(128, -1).astype(np.float32)
def f(rng, *shape):
    return mx_ref.flush((rng.standard_normal(shape, dtype=np.float32) * np.exp2(rng.integers(-2, 3, shape[:-1] + (1,)))).astype(BF))
def wide(rng, *shape, cols=0):
    v = rng.standard_normal(shape, dtype=np.float32) * np.exp2(rng.integers(-12, 13, shape)).astype(np.float32)
    if cols: v *= np.repeat(np.exp2(rng.integers(-cols, cols + 1, shape[:-2] + (1, shape[-1] // 4))) * (rng.random(shape[:-2] + (1, shape[-1] // 4)) > 0.0625), 4, axis=-1).astype(np.float32)
    return mx_ref.flush(v.astype(BF))
C, K, R = 256, 128, 3
def big(v):
    v = v.astype(np.float32)
    v[np.abs(v) < np.float32(2.0 ** -16)] = 0
    return v.astype(BF)
def numbers_of(rng):
    return {"x": np.array(f(rng, N, 128, 4 * C)), "u": np.array(f(rng, N, 128, 512)), "v": np.array(f(rng, N, 128, 512))}
def bindings(rng):
    return np.stack([gtable(np.argsort(rng.random((8, C)), axis=1)) for r in range(N)])
def targets(rng):
    return np.stack([gtable(rng.integers(0, C, (8, C))) for r in range(N)])
def layers(rng):
    return np.clip(f(rng, N, 128, 2048).astype(np.float32), -1.75, 1.75).astype(BF).reshape(N, 8, 16, 4, 8, 16, 4)
def planted(rng, quiet, pairs):
    w = layers(rng)
    w[:, :, :, :, :, quiet] = 0
    for a, b in pairs:
        for g in range(8): w[:, g, a, 0, g, b, 0] = 1
    return w
def weights(rng, w):
    c, p = packed(np.ascontiguousarray(w).reshape(N, 128, 2048), rng)
    return {"wc": c, "ws": p}
def setup_inputs(rng):
    return {**numbers_of(rng), "bd": bindings(rng), "ds": targets(rng), **weights(rng, layers(rng))}
def setup_inputs_ties(rng):
    d = numbers_of(rng)
    x = d["x"].reshape(N, 8, 16, C, 4)
    x[:, :, 0] = 0
    x[:, :, 0, :, 0] = rng.integers(-1, 2, (N, 8, C)).astype(np.float32).astype(BF)
    u = d["u"].reshape(N, 128, 128, 4)
    u[:, :, ::16] = 0
    o = rng.permutation(N)
    for r in range(N):
        for h in range(0, 128, 16): u[r, h + 1, h, 0] = 0.0 if r == o[0] else -1.0 if r == o[1] else 1.0
    return {"x": x.reshape(N, 128, 4 * C), "u": u.reshape(N, 128, 512), "v": d["v"], "bd": bindings(rng), "ds": targets(rng), **weights(rng, planted(rng, [0, 1], [(0, 1)]))}
def setup_inputs_near(rng):
    d = numbers_of(rng)
    x = d["x"].astype(np.float32).reshape(N, 8, 16, C, 4)
    x[:, :, :6] = 0
    x[:, :, 8:] = 0
    x[:, :, 0, :, 0] = 1
    x[:, :, 1, :, 0] = 1
    x[:, :, 4, :, 0] = rng.integers(-8, 9, (N, 8, C)) * 0.125
    x[:, :, 8, :, 0] = rng.integers(-8, 9, (N, 8, C)) * 2.0 ** -17
    u = d["u"].reshape(N, 128, 128, 4)
    u[:, :, ::16] = 0
    o = rng.permutation(N) % 4
    for r in range(N):
        c = np.where(rng.permutation(8) < 2, 1.0, -1.0)
        k = 1.0 if o[r] == 0 else 2.0 ** -12
        for h in range(0, 128, 16):
            if o[r] < 2:
                u[r, h + 2, h, 0] = c[h // 16] * k
                u[r, h + 3, h, 0] = c[h // 16] * k * 2.0 ** -10
                u[r, h + 10, h, 0] = k * 2.0 ** -4
            elif o[r] == 2:
                u[r, h + 10, h, 0] = 1.125 * 2.0 ** -30
                u[r, h + 11, h, 0] = -2.0 ** -30
            else:
                u[r, h + 5, h, 0] = 1.0
                u[r, h + 10, h, 0] = 1.0
    w = planted(rng, [0, 1, 2, 3, 4, 5, 8, 9, 10, 11, 12, 13, 14, 15], [(0, 2), (1, 3), (4, 5), (8, 10), (8, 11)])
    return {"x": x.reshape(N, 128, 4 * C).astype(BF), "u": u.reshape(N, 128, 512), "v": d["v"], "bd": bindings(rng), "ds": targets(rng), **weights(rng, w)}
def setup_inputs_ends(rng):
    d = numbers_of(rng)
    o = (np.arange(N) + rng.integers(N)) % N
    few = N // 4
    x = 2.0 ** 20 * (1 - 0.125 * rng.integers(0, 2, (N, 1, C, 1))) * np.ones((1, 128, 1, 4))
    c = 2.0 ** -30 * rng.choice([-1.0, 1.0], (128, 1, 4))
    less = rng.permutation(8) % 2 == 0
    u = d["u"].reshape(N, 128, 128, 4)
    v = rng.choice([-1.0, 1.0], (N, 128, 512))
    w = np.where(rng.random((N, 128, 512, 4)) < rng.random((N, 1, 512, 1)), 1.5, 1.75).reshape(N, 128, 2048)
    e, t = bindings(rng), np.zeros((N, 8, C), int)
    e[o[0]] = gtable(np.stack([np.arange(C)[::-1]] * 8))
    e[o[few]] = gtable(np.stack([np.arange(C)] * 8))
    for i in range(N):
        r = o[i]
        v[r] *= 2.0 ** 30 if i % 2 == 1 else 2.0 ** -30
        s = np.full(8, -1.0)
        if i == few:
            s = np.where(less, -1.0, 1.0)
            t[r][~np.roll(less, 1)] = C - 1
        u[r, :, ::16] = (s * (2.0 ** -30 if i < few else 2.0 ** 30)).astype(np.float32).astype(BF)[None, :, None]
        if i < few:
            x[r] = c
            t[r] = C - 1
            w[o[i + 1]] = 0
    return {"x": x.astype(np.float32).reshape(N, 128, 4 * C).astype(BF), "u": u.reshape(N, 128, 512), "v": v.astype(np.float32).astype(BF), "bd": e, "ds": np.stack([gtable(t[r]) for r in range(N)]), **weights(rng, w.astype(np.float32).astype(BF))}
def setup_inputs_odd(rng):
    d = numbers_of(rng)
    n = (N, 8, 16, C, 4)
    x = (1 + (2 * rng.integers(0, 64, n) + 1) * 2.0 ** -7) * np.exp2(-rng.integers(8, 15, n).astype(np.float64)) * rng.choice([-1.0, 1.0], n)
    x[:, :, ::8, :, 0] = rng.choice([1.96875, 1.875], (N, 8, 2, C))
    x[:, :, 9, :, 0] = 1.875
    x[:, :, 10, :, 0] = 0.09375
    x[:, :, 11, :, 0] = rng.integers(-15, 16, (N, 8, C)) * 0.125
    u = d["u"].reshape(N, 128, 128, 4)
    u[:, :, ::16] = 0
    for h in range(0, 128, 16): u[:, h + 13, h, 0] = 1.0
    w = planted(rng, [8, 9, 10, 11, 12, 13, 14, 15], [(9, 12), (10, 12), (11, 13)])
    for g in range(8): w[:, g, 11, 0, g, 13, 0] = 2.0 ** -12
    return {"x": x.astype(np.float32).reshape(N, 128, 4 * C).astype(BF), "u": u.reshape(N, 128, 512), "v": d["v"], "bd": bindings(rng), "ds": targets(rng), **weights(rng, w)}
def setup_inputs_spread(rng):
    d = setup_inputs(rng)
    d["x"] = big(wide(rng, N, 128, 4 * C, cols=4))
    return d
def check_inputs(d):
    b = []
    for k, m in (("x", 20), ("u", 30), ("v", 30)):
        a = np.abs(d[k].astype(np.float32))
        if not (np.isfinite(a).all() and ((a == 0) | (a >= 2.0 ** -30) & (a <= 2.0 ** m)).all()): b.append("a value of " + k)
    if not ((d["ds"] >= 0) & (d["ds"] < C)).all(): b.append("an entry of ds")
    none, least, most = [emit(mx_ref.quantize(np.full((128, 16), k, np.float32).astype(BF)))[1][0, 0] for k in (0.0, 2.0 ** -30, 1.75)]
    for r in range(N):
        if (np.sort(gentries(d["bd"][r]), axis=1) != np.arange(C)).any(): b.append("bd: not every port once in a group")
        if ((d["wc"][r] == 0x7F) | (d["wc"][r] == 0xFF)).any(): b.append("wc: a code that is no number")
        s = mx_ref.live(d["ws"][r])
        if ((s != none) & ((s < least) | (s > most))).any(): b.append("ws: a scale out of range")
        if (((d["wc"][r].reshape(16, 8, 512, 4) & 0x7F) != 0) & (s == none)[:, None, :, None]).any(): b.append("wc: a number other than zero at the scale of zeros")
        if not (np.abs(decode(pk(d["wc"][r], d["ws"][r]))) <= 1.75).all(): b.append("wc and ws: a number beyond 1.75 in size")
    return b
def reference(x, u, v, bd, ds, wc, ws):
    qu = [mx_ref.quantize(u[r]) for r in range(N)]
    lay = [pk(wc[r], ws[r]) for r in range(N)]
    now = [x[r] for r in range(N)]
    port = np.stack([gentries(bd[r]) for r in range(N)]).astype(np.int64)
    aim = np.stack([gentries(ds[r]) for r in range(N)]).astype(np.int64)
    for step in range(R):
        iv = np.argsort(port, axis=2)
        m = np.take_along_axis(iv, aim, axis=2)
        own = [decode(mx_ref.quantize(now[r])).astype(BF) for r in range(N)]
        z = [((own[r].astype(np.float32) + gcols(own[r], m[r]).astype(np.float32)) * np.float32(0.5)).astype(BF) for r in range(N)]
        out = [mx_ref.quantize(gcols(z[r], iv[r][:, K:])) for r in range(N)]
        reply = []
        for r in range(N):
            met = ((decode(out[(r - 1) % N]) + gcols(own[r], iv[r][:, :K]).astype(np.float32)) * np.float32(0.5)).astype(BF)
            q = mx_ref.quantize(met)
            reply.append(mx_ref.quantize(tile([mx_ref.matmul(pick(lay[r], np.arange(128 * b, 128 * b + 128)), q) * np.float32(0.0078125) for b in range(4)])))
        for r in range(N):
            q = reply[(r + 1) % N]
            back = gcols(decode(q).astype(BF), np.where(port[r] < K, -1, port[r] - K))
            now[r] = (z[r].astype(np.float32) + back.astype(np.float32)).astype(BF)
            s = mx_ref.matmul(qu[r], q)[::16] + np.float32(0.0)
            place = np.argsort(np.argsort(s, axis=1, kind="stable"), axis=1)
            for g in range(8):
                h = (g + 1) % 8
                k = np.nonzero(s[g] <= 0)[0]
                low, high = iv[r, h, place[g, k]], iv[r, h, K + k]
                port[r, h, low] = K + k
                port[r, h, high] = place[g, k]
    y, ob = np.zeros((N, 128, C), np.float32), np.zeros((N, 8, C), np.float32)
    oc, osc = np.zeros((N, 128, 4 * C), np.uint8), np.zeros((N, 16, C), np.uint8)
    for r in range(N):
        q = mx_ref.quantize(now[r])
        y[r] = mx_ref.matmul(mx_ref.quantize(v[r]), q)
        ob[r] = port[r]
        oc[r], osc[r] = emit(q)
    return {"y": y, "ob": ob, "oc": oc, "osc": osc}

from concourse.mybir import dt, AluOpType, ActivationFunctionType

ALU = AluOpType
ACT = ActivationFunctionType
BF, F32, I32, U16, U8, X4 = "bfloat16", "float32", "int32", "uint16", "uint8", "float8_e4m3fn_x4"
N, C, K, R = 8, 256, 128, 3
OPT = {"chunks": ((0, 4), (4, 8)), "abs": (), "pre": 2, "post": 0}
SEG = 132


def _scratch():
    s = {}

    def sb(name, n, d):
        s[name] = ("sbuf", [128, n], d)

    def mx(name, n):
        sb(name + "c", n, X4)
        sb(name + "s", n, U8)

    sb("xt", 1024, BF); sb("ut", 512, BF); sb("vt", 512, BF)
    sb("bdi", 16, I32); sb("dsi", 16, I32)
    for name, n in (("w", 512), ("u", 128), ("up", 128), ("v", 128), ("e", 1024), ("x0", 256), ("xf", 256)):
        mx("q" + name, n)
    sb("eh", 520, BF); sb("e1", 520, BF)
    sb("id3", 384, BF); sb("jm16", 256, BF); sb("jm4", 128, BF)
    sb("m16", 256, BF); sb("k16", 256, BF); sb("m4", 128, BF); sb("k4", 128, BF)
    sb("pi", 8, I32); sb("pf", 8, F32); sb("ul", 8, U16)
    sb("tau", 8 * SEG, BF); sb("ge", 8 * SEG, BF); sb("so", 8 * SEG, BF)
    sb("sgn", 1024, BF); sb("acc", 8, F32); sb("mskf", 128, F32); sb("swf", 128, F32)
    sb("sg", 4 * 384, BF); sb("ub", 3 * 256, BF); sb("tb", 2 * 256, BF)
    sb("mk", 8 * 256, BF); sb("sc", 8 * 256, BF)
    sb("sig", 4 * 16, U16); sb("tw", 3 * 16, U16); sb("pw", 4 * 16, U16); sb("b4", 6 * 32, U16)
    sb("pt", 64, F32)
    sb("xp", 1024, BF); sb("xf", 1024, BF); sb("yo", 256, F32); sb("obf", 256, F32)
    for r in range(R):
        sb("fh%d" % r, 1024, BF)
        for name in ("gah", "gal", "zh", "zl", "vv", "hh"):
            sb("%s%d" % (name, r), 512, BF)
        for name in ("m", "lm", "vq", "h", "lh"):
            mx("q%s%d" % (name, r), 128)
        if r < R - 1:
            sb("xh%d" % r, 512, BF)
            mx("qxl%d" % r, 128); mx("qxh%d" % r, 128)
    s["ps"] = ("psum", [128, 4096], F32)
    return s


SCRATCH = _scratch()
LOADS = ["bd", "ds", "x", "wc", "ws", "u", "v"]
SEMAPHORES = (["ld_" + n for n in LOADS] + ["am%d" % r for r in range(R)] + ["ah%d" % r for r in range(R)]
              + ["cg", "ct", "sent", "cv", "ca", "stored"])


def rank_program(g, core, T, topo):
    rank = T.rank_of(core)
    if rank is None:
        return
    nxt, prv = T.cores[(rank + 1) % N], T.cores[(rank - 1) % N]
    Q = {"v": g.vector, "a": g.scalar, "t": g.tensor, "g": g, "s": g.sync}
    own = {"v": "cv", "a": "ca", "t": "ct", "g": "cg"}
    total = {n: 0 for n in SEMAPHORES}
    known = {q: {} for q in Q}
    writer, readers, waited = {}, {}, {}

    def order(q, rd, wr):
        deps = []
        for t in rd:
            if t in writer:
                deps.append(writer[t])
            if t.startswith("ps"):
                deps += [d for d in readers.get(t, []) if d[3] != q]
        for t in wr:
            if t in writer:
                deps.append(writer[t])
            deps += readers.get(t, [])
        deps = [d for i, d in enumerate(deps)
                if not any(j != i and e[2].get(d[0], 0) >= d[1] and (e[0], e[1]) != (d[0], d[1]) for j, e in enumerate(deps))]
        for sem, val, clock, _q in deps:
            if known[q].get(sem, 0) < val:
                Q[q].wait_ge(T.sem[sem], val)
                waited[sem] = max(waited.get(sem, 0), val)
                for k, x in clock.items():
                    known[q][k] = max(known[q].get(k, 0), x)

    def note(q, sem, val, rd, wr):
        clock = dict(known[q])
        clock[sem] = val
        d = (sem, val, clock, q)
        for t in rd:
            readers.setdefault(t, []).append(d)
        for t in wr:
            writer[t] = d
            readers[t] = []

    def op(q, call, rd, wr):
        order(q, rd, wr)
        total[own[q]] += 1
        call().then_inc(T.sem[own[q]], 1)
        note(q, own[q], total[own[q]], rd, wr)

    def dma(q, sem, out, in_, rd, wr):
        order(q, rd, wr)
        total[sem] += 16
        Q[q].dma_start(out, in_).then_inc(T.sem[sem], 16)
        note(q, sem, total[sem], rd, wr)

    V, A, PE = g.vector, g.scalar, g.tensor
    ps = T.ps

    def bank(b, n):
        return ps[:, 512 * b:512 * b + n]

    def vcopy(out, in_, rd, wr):
        op("v", lambda: V.tensor_copy(out, in_), rd, wr)

    def acopy(out, in_, rd, wr):
        op("a", lambda: A.activation(out, in_, ACT.Copy), rd, wr)

    def tt(out, a, b, alu, rd, wr):
        op("v", lambda: V.tensor_tensor(out, a, b, alu), rd, wr)

    def ts(out, a, s1, o1, rd, wr, s2=None, o2=None):
        if o2 is None:
            op("v", lambda: V.tensor_scalar(out, a, s1, None, o1), rd, wr)
        else:
            op("v", lambda: V.tensor_scalar(out, a, s1, s2, o1, o2), rd, wr)

    def scan(out, d0, d1, rd, wr):
        op("v", lambda: V.tensor_tensor_scan(out, d0, d1, 0.0, ALU.mult, ALU.add), rd, wr)

    def fill(ap, c, rd, wr):
        op("v", lambda: V.memset(ap, c), rd, wr)

    def quant(name, a, b, tile, rd, tok=None):
        op("v", lambda: V.quantize_mx(T[name + "c"][:, a:b], T[name + "s"][:, a:b], tile), rd, [tok or name])

    def mm(b, n, w, w0, x, rd):
        op("t", lambda: PE.matmul_mx(bank(b, n), T[w + "c"][:, w0:w0 + 128], T[w + "s"][:, w0:w0 + 128],
                                     T[x + "c"][:, 0:n], T[x + "s"][:, 0:n], True, True), rd, ["ps%d" % b])

    def send(dst, src, land, sem):
        order("g", [src], [])
        rid, pid = topo.addr(dst)[0:2]
        m = topo.mask(core, dst)
        g.remote_dma(T[land + "c"][:].bitcast(dt.uint8), T[src + "c"][:].bitcast(dt.uint8), T.sem[sem], T.sem.sent, pid, rid, m)
        g.remote_dma(T[land + "s"][:], T[src + "s"][:], T.sem[sem], T.sem.sent, pid, rid, m)
        total["sent"] += 2 * len(topo.engines(core, dst))

    def arrival(src, land, sem):
        total[sem] = 2 * len(topo.engines(src, core))
        writer[land] = (sem, total[sem], {sem: total[sem]}, "r")

    slot = [0]

    def wrap(table, rd, n, four):
        i = slot[0] % 8
        slot[0] += 1
        mk, sc = T.mk[:, 256 * i:256 * i + n], T.sc[:, 256 * i:256 * i + n]
        m, k = (T.m4, T.k4) if four else (T.m16, T.k16)
        tt(mk, table, m[:, 0:n], ALU.mult, rd + ["m4" if four else "m16"], ["mk%d" % i])
        scan(sc, k[:, 0:n], mk, ["mk%d" % i, "k4" if four else "k16"], ["sc%d" % i])
        step = 4 if four else 16
        return T.sc[:, 256 * i + step - 1:256 * i + n:step], "sc%d" % i

    idv, idm = T.id3[:, 128:384], T.id3[:, 0:256]

    def sg_lo(r):
        return T.sg[:, 0:128] if r == 0 else T.sg[:, 384 * r + 128:384 * r + 256]

    def sig(r, half):
        return T.sig[:, 16 * r + 8 * half:16 * r + 8 * half + 8]

    def partners(r, half):
        view, tok = wrap(T.ub[:, 256 * r:256 * r + 256].indirect(sig(r, half)), ["ub%d" % r, "sig%d_%d" % (r, half)], 128, True)
        o = 32 * (2 * r + half)
        ts(T.b4[:, o:o + 32], view, T.pf[:, 3:4], ALU.add, [tok, "pf3"], ["b4_%d_%d" % (r, half)])
        return T.b4[:, o:o + 32]

    def fh_all(r):
        return ["fh%d_%d_%d" % (r, b, h) for b in range(4) for h in range(2)]

    def first_columns(r, half, planes):
        name = ("gal%d", "gah%d")[half] % r
        for b in planes:
            acopy(T[name][:, b:512:4], T["fh%d" % r][:, 256 * b:256 * b + 256].indirect(sig(r, half)),
                  ["fh%d_%d_0" % (r, b), "fh%d_%d_1" % (r, b), "sig%d_%d" % (r, half)], ["%s_%d" % (name, b)])

    def four(name):
        return ["%s_%d" % (name, b) for b in range(4)]

    dma("a", "ld_bd", T.bdi[:], T.bd[:], [], ["bdi"])
    dma("a", "ld_ds", T.dsi[:], T.ds[:], [], ["dsi"])
    dma("s", "ld_x", T.xt[:], T.x[:], [], ["xt"])
    dma("s", "ld_wc", T.qwc[:].bitcast(dt.uint8), T.wc[:], [], ["qw_c"])
    dma("s", "ld_ws", T.qws[:], T.ws[:], [], ["qw_s"])
    dma("s", "ld_u", T.ut[:], T.u[:], [], ["ut"])
    dma("s", "ld_v", T.vt[:], T.v[:], [], ["vt"])
    for r in range(R):
        arrival(prv, "qlm%d" % r, "am%d" % r)
        arrival(nxt, "qlh%d" % r, "ah%d" % r)

    def iota(out, pattern, cm, wr, small=True):
        if small:
            op("g", lambda: g.iota(out, pattern, 0, cm, allow_small_or_imprecise_dtypes=True), [], wr)
        else:
            op("g", lambda: g.iota(out, pattern, 0, cm), [], wr)

    iota(T.pi[:, 0:1], [[1, 1]], 1, ["pi0"], False)
    iota(T.pf[:, 0:1], [[1, 1]], 1, ["pf0"])
    iota(idv, [[1, 256]], 0, ["idv"])
    iota(T.jm4[:], [[0, 32], [1, 4]], 0, ["jm4"])
    iota(T.jm16[:], [[0, 16], [1, 16]], 0, ["jm16"])
    fill(T.eh[:], 0.0, [], ["eh"])
    ts(T.pi[:, 1:2], T.pi[:, 0:1], 15, ALU.bitwise_and, ["pi0"], ["pi1"])
    ts(T.pi[:, 2:3], T.pi[:, 0:1], 2, ALU.arith_shift_right, ["pi0"], ["pi2"], 3, ALU.bitwise_and)
    ts(T.pi[:, 3:4], T.pi[:, 0:1], 3, ALU.bitwise_and, ["pi0"], ["pi3"])
    vcopy(T.pf[:, 1:3], T.pi[:, 1:3], ["pi1", "pi2"], ["pf1"])
    ts(T.pf[:, 3:4], T.pi[:, 3:4], 256.0, ALU.mult, ["pi3"], ["pf3"])
    ts(T.eh[:, 3:515:4], T.id3[:, 128:256], T.pf[:, 0:1], ALU.is_equal, ["idv", "pf0"], ["eh"], 0.5, ALU.mult)
    for b in range(4):
        quant("qe", 128 * b, 128 * b + 128, T.eh[:, 3 - b:515 - b], ["eh"], "qe%d" % b)
    op("a", lambda: A.activation(T.k4[:], T.jm4[:], ACT.Sign), ["jm4"], ["k4"])
    op("a", lambda: A.activation(T.k16[:], T.jm16[:], ACT.Sign), ["jm16"], ["k16"])
    ts(T.m4[:], T.jm4[:], T.pf[:, 2:3], ALU.is_equal, ["jm4", "pf1"], ["m4"])
    ts(T.m16[:], T.jm16[:], T.pf[:, 1:2], ALU.is_equal, ["jm16", "pf1"], ["m16"])

    def later_constants():
        ts(T.e1[:], T.eh[:], 2.0, ALU.mult, ["eh"], ["e1"])
        for b in range(4):
            quant("qe", 512 + 128 * b, 640 + 128 * b, T.e1[:, 3 - b:515 - b], ["e1"], "qe%d" % (4 + b))
        fill(T.tau[:], 1.0, [], ["tau"])
        for c in range(8):
            o = SEG * c + 16 * c
            op("a", lambda: A.activation(T.tau[:, o:o + 16], T.m16[:, 0:16], ACT.Identity, bias=1.0, scale=-2.0), ["m16", "tau"], ["tau_d%d" % c])
        e = 8 * SEG
        ts(T.ge[:, 130:e:SEG], T.id3[:, 256:384:16], T.pf[:, 1:2], ALU.add, ["idv", "pf1"], ["ge_k"])
        fill(T.ge[:, 129:e:SEG], -256.0, [], ["ge_c"])
        fill(T.ge[:, 131:e:SEG], 0.0, [], ["ge_z"])
        fill(T.tau[:, 0:e:SEG], 0.0, ["tau", "tau_d0"], ["tau_0"])
        ts(T.ul[:, 1:8], T.id3[:, 128:240:16], 0.0, ALU.add, ["idv"], ["ul1"])
        fill(T.ul[:, 0:1], 112, [], ["ul0"])
        quant("qu", 0, 128, T.ut[:], ["ut"])
        vcopy(T.qupc[:].bitcast(dt.uint32), T.quc[:].bitcast(dt.uint32).indirect(T.ul[:]), ["qu", "ul0", "ul1"], ["qup_c"])
        acopy(T.qups[:], T.qus[:].indirect(T.ul[:]), ["qu", "ul0", "ul1"], ["qup_s"])

    TAU = ["tau", "tau_0", "tau_f"] + ["tau_d%d" % c for c in range(8)] + ["ge_k", "ge_c", "ge_z"]

    vcopy(T.pw[:, 48:64], T.bdi[:], ["bdi"], ["pwn"])
    vcopy(T.sg[:, 0:256].indirect(T.pw[:, 48:64]), idv, ["pwn", "idv"], ["sg0_lo", "sg0_hi"])
    vcopy(T.tw[:, 0:16], T.dsi[:], ["dsi"], ["tw0"])
    quant("qx0", 0, 256, T.xt[:], ["xt"])
    for b in range(4):
        mm(b, 256, "qe", 128 * b, "qx0", ["qe%d" % b, "qx0"])
    acopy(T.ub[:, 0:256], T.sg[:, 0:256].indirect(T.tw[:, 0:16]), ["sg0_lo", "sg0_hi", "tw0"], ["ub0"])
    view, tok = wrap(T.sg[:, 128:256], ["sg0_hi"], 128, False)
    vcopy(sig(0, 1), view, [tok], ["sig0_1"])
    for b in (0, 1):
        acopy(T.fh0[:, 256 * b:256 * b + 256], bank(b, 256), ["ps%d" % b], ["fh0_%d_0" % b, "fh0_%d_1" % b])
    high = partners(0, 1)
    for b in (2, 3):
        vcopy(T.fh0[:, 256 * b:256 * b + 256], bank(b, 256), ["ps%d" % b], ["fh0_%d_0" % b, "fh0_%d_1" % b])
    first_columns(0, 1, range(4))

    def places(r, between):
        tt(T.mskf[:], bank(4, 128), T.m16[:, 0:128], ALU.mult, ["ps4", "m16"], ["mskf"])
        scan(T.swf[:], T.k16[:, 0:128], T.mskf[:], ["mskf", "k16"], ["swf"])
        chunks, by_scalar = OPT["chunks"], OPT["abs"]

        def signs(lo, hi):
            for c in range(lo, hi):
                op("a", lambda: A.activation(T.sgn[:, 128 * c:128 * c + 128], bank(4, 128), ACT.Sign, bias=T.swf[:, 16 * c + 15:16 * c + 16],
                                             scale=-1.0, accum_out=T.acc[:, c:c + 1]), ["ps4", "swf"], ["sgn%d" % c, "acc%d" % c])
            for c in range(lo, hi):
                if c in by_scalar:
                    op("a", lambda: A.activation(T.ge[:, SEG * c:SEG * c + 128], T.sgn[:, 128 * c:128 * c + 128], ACT.Abs), ["sgn%d" % c], ["ge%d" % c])
            acopy(T.ge[:, SEG * lo + 128:SEG * hi:SEG], T.acc[:, lo:hi], ["acc%d" % c for c in range(lo, hi)], ["ge_a%d" % lo])

        def count(lo, hi):
            for c in range(lo, hi):
                if c not in by_scalar:
                    ts(T.ge[:, SEG * c:SEG * c + 128], T.sgn[:, 128 * c:128 * c + 128], 0.0, ALU.not_equal, ["sgn%d" % c], ["ge%d" % c])
            scan(T.so[:, SEG * lo:SEG * hi], T.tau[:, SEG * lo:SEG * hi], T.ge[:, SEG * lo:SEG * hi],
                 TAU + ["ge_a%d" % lo] + ["ge%d" % c for c in range(lo, hi)], ["so%d" % lo])

        ts(T.tau[:, 130:8 * SEG:SEG], T.swf[:, 15:128:16], 0.0, ALU.is_le, ["swf", "tau"], ["tau_f"], 0.5, ALU.mult)
        between(lambda: [signs(lo, hi) for lo, hi in chunks])
        for lo, hi in chunks:
            count(lo, hi)
        vcopy(sig(r, 1), T.so[:, 130:8 * SEG:SEG], ["so%d" % lo for lo, hi in chunks], ["sig%d_1" % r])
        o = 384 * r
        vcopy(T.sg[:, o + 128:o + 384].indirect(sig(r, 1)), T.id3[:, 256:384], ["sig%d_1" % r, "idv"], ["sg%d_lo" % r])
        acopy(T.sg[:, o:o + 128], idv.indirect(sig(r, 1)), ["sig%d_1" % r, "idv"], ["sg%d_hi" % r])

    def ports(r):
        if r == 0:
            src, tok = T.bdi[:], "bdi"
        else:
            o = 384 * r
            src, tok = wrap(T.sg[:, o:o + 256].indirect(T.pw[:, 16 * r - 16:16 * r]), ["sg%d_lo" % r, "sg%d_hi" % r, "pw%d" % (r - 1)], 256, False)
        ts(T.pt[:, 0:16], src, 128.0, ALU.is_ge, [tok], ["pt0"], -256.0, ALU.mult)
        tt(T.pt[:, 16:32], T.pt[:, 0:16], src, ALU.add, [tok, "pt0"], ["pt1"])
        ts(T.pw[:, 16 * r:16 * r + 16], T.pt[:, 16:32], 128.0, ALU.add, ["pt1"], ["pw%d" % r])

    for r in range(R):
        last = r == R - 1
        fh, zh = T["fh%d" % r], T["zh%d" % r]
        tt(zh[:], fh[:].indirect(high), T["gah%d" % r][:], ALU.add, fh_all(r) + four("gah%d" % r) + ["b4_%d_1" % r], ["zh%d" % r])
        quant("qm%d" % r, 0, 128, zh[:], ["zh%d" % r])
        send(nxt, "qm%d" % r, "qlm%d" % r, "am%d" % r)
        view, tok = wrap(sg_lo(r), ["sg%d_lo" % r], 128, False)
        vcopy(sig(r, 0), view, [tok], ["sig%d_0" % r])
        first_columns(r, 0, range(4))
        low = partners(r, 0)
        both = ["sig%d_0" % r, "sig%d_1" % r]
        if r == 0:
            vcopy(T.id3[:, 0:128], T.id3[:, 256:384], ["idv"], ["idm"])
            acopy(T.tb[:, 0:256], idm.indirect(T.tw[:, 0:16]), ["idm", "idv", "tw0"], ["tb0"])
            later_constants()
        else:
            ports(r)
        vv, hh = T["vv%d" % r], T["hh%d" % r]
        for b in range(4):
            mm(b, 128, "qe", 128 * b, "qlm%d" % r, ["qe%d" % b, "qlm%d" % r])
            tt(vv[:, b:512:4], bank(b, 128), T["gal%d" % r][:, b:512:4], ALU.add, ["ps%d" % b, "gal%d_%d" % (r, b)], ["vv%d_%d" % (r, b)])
        quant("qvq%d" % r, 0, 128, vv[:], four("vv%d" % r))
        for b in range(4):
            mm(4 + b, 128, "qw", 128 * b, "qvq%d" % r, ["qw_c", "qw_s", "qvq%d" % r])
            if b % 2 == 0:
                op("a", lambda: A.activation(hh[:, b:512:4], bank(4 + b, 128), ACT.Identity, scale=0.0078125), ["ps%d" % (4 + b)], ["hh%d_%d" % (r, b)])
            else:
                ts(hh[:, b:512:4], bank(4 + b, 128), 0.0078125, ALU.mult, ["ps%d" % (4 + b)], ["hh%d_%d" % (r, b)])
        quant("qh%d" % r, 0, 128, hh[:], four("hh%d" % r))
        send(prv, "qh%d" % r, "qlh%d" % r, "ah%d" % r)
        o = 384 * (r + 1)
        if not last:
            zl, nf = T["zl%d" % r], T["fh%d" % (r + 1)]
            tt(zl[:], fh[:].indirect(low), T["gal%d" % r][:], ALU.add, fh_all(r) + four("gal%d" % r) + ["b4_%d_0" % r], ["zl%d" % r])
            quant("qxl%d" % r, 0, 128, zl[:], ["zl%d" % r])
            for b in range(4):
                mm(b, 128, "qe", 128 * b, "qxl%d" % r, ["qe%d" % b, "qxl%d" % r])
            src = T.tb[:, 256 * r:256 * r + 256].indirect(T.sig[:, 16 * r:16 * r + 16])
            if r == 0:
                acopy(T.tb[:, 256:512], src, ["tb0"] + both, ["tb1"])
            for b in range(4):
                acopy(nf[:, 256 * b:256 * b + 128], bank(b, 128), ["ps%d" % b], ["fh%d_%d_0" % (r + 1, b)])
            view, tok = wrap(src, ["tb%d" % r] + both, 256, False)
            vcopy(T.tw[:, 16 * r + 16:16 * r + 32], view, [tok], ["tw%d" % (r + 1)])
            vcopy(T.sg[:, o + 128:o + 384], idv, ["idv"], ["sg%d_lo" % (r + 1)])
            if r == 0:
                ports(0)
            else:
                quant("qv", 0, 128, T.vt[:], ["vt"])
        else:
            tt(T.zl2[:], fh[:].indirect(low), T["gal%d" % r][:], ALU.add, fh_all(r) + four("gal%d" % r) + ["b4_%d_0" % r], ["xf_t"])
            for b in range(4):
                acopy(T.xp[:, 256 * b + 128:256 * b + 256], T.zl2[:, b:512:4], ["xf_t"], ["xp%d_0" % b])
            vcopy(T.sg[:, o + 128:o + 384], idv, ["idv"], ["sg%d_lo" % (r + 1)])
        mm(4, 128, "qup", 0, "qlh%d" % r, ["qup_c", "qup_s", "qlh%d" % r])
        for b in range(4):
            mm(b, 128, "qe", 512 + 128 * b, "qlh%d" % r, ["qe%d" % (4 + b), "qlh%d" % r])
        if not last:
            def update(signs):
                xh = T["xh%d" % r]
                signs()
                for b in range(4):
                    tt(xh[:, b:512:4], bank(b, 128), zh[:, b:512:4], ALU.add, ["ps%d" % b, "zh%d" % r], ["xh%d_%d" % (r, b)])
                quant("qxh%d" % r, 0, 128, xh[:], four("xh%d" % r))
                for b in range(4):
                    mm(b, 128, "qe", 128 * b, "qxh%d" % r, ["qe%d" % b, "qxh%d" % r])
                for b in range(4):
                    acopy(nf[:, 256 * b + 128:256 * b + 256], bank(b, 128), ["ps%d" % b], ["fh%d_%d_1" % (r + 1, b)])
            places(r + 1, update)
            first_columns(r + 1, 1, range(4))
            vcopy(T.ub[:, 256 * (r + 1):256 * (r + 2)], T.sg[:, o:o + 256].indirect(T.tw[:, 16 * r + 16:16 * r + 32]),
                  ["sg%d_lo" % (r + 1), "sg%d_hi" % (r + 1), "tw%d" % (r + 1)], ["ub%d" % (r + 1)])
            high = partners(r + 1, 1)
        else:
            pw = T.pw[:, 16 * r:16 * r + 16]

            def finish(signs):
                for b in range(4):
                    tt(T.xp[:, 256 * b:256 * b + 128], bank(b, 128), zh[:, b:512:4], ALU.add, ["ps%d" % b, "zh%d" % r], ["xp%d_1" % b])
                def plane(cp, b):
                    cp(T.xf[:, b:1024:4], T.xp[:, 256 * b:256 * b + 256].indirect(pw), ["xp%d_0" % b, "xp%d_1" % b, "pw%d" % r], ["xf_%d" % b])
                for b in range(OPT["pre"]):
                    plane(acopy, b)
                for b in range(OPT["pre"], 4 - OPT["post"]):
                    plane(vcopy, b)
                signs()
                for b in range(4 - OPT["post"], 4):
                    plane(acopy, b)
                quant("qxf", 0, 256, T.xf[:], four("xf"))
                mm(5, 256, "qv", 0, "qxf", ["qv", "qxf"])
                dma("s", "stored", T.oc[:], T.qxfc[:].bitcast(dt.uint8), ["qxf"], [])
                for k in range(4):
                    dma("s", "stored", T.osc[4 * k:4 * k + 4, :], T.qxfs[32 * k:32 * k + 4, :], ["qxf"], [])
                acopy(T.yo[:], bank(5, 256), ["ps5"], ["yo"])
                dma("s", "stored", T.y[:], T.yo[:], ["yo"], [])
            places(r + 1, finish)
            rd = ["sg%d_lo" % (r + 1), "sg%d_hi" % (r + 1), "pw%d" % r]
            vcopy(T.obf[:, 0:128], T.sg[:, o:o + 256].indirect(T.pw[:, 16 * r:16 * r + 8]), rd, ["ob0"])
            acopy(T.obf[:, 128:256], T.sg[:, o:o + 256].indirect(T.pw[:, 16 * r + 8:16 * r + 16]), rd, ["ob1"])
            dma("s", "stored", T.ob[:], T.obf[0:128:16, :], ["ob0", "ob1"], [])

    for sem in SEMAPHORES:
        if total[sem] > waited.get(sem, 0):
            g.wait_ge(T.sem[sem], total[sem])
